import numpy as np
import ml_dtypes


def mxq(x, axis, fmt="e4m3"):
    dtype, down = {"e4m3": (ml_dtypes.float8_e4m3fn, 7), "e5m2": (ml_dtypes.float8_e5m2, 14)}[fmt]
    v = np.moveaxis(np.asarray(x, np.float32).astype(ml_dtypes.bfloat16).astype(np.float64), axis, -1)
    blocks = v.reshape(v.shape[:-1] + (-1, 32))
    amax = np.abs(blocks).max(-1, keepdims=True)
    byte = np.maximum(np.where(amax > 0, np.frexp(amax)[1] - 1 + 127, 0) - down, 1)
    scale = np.exp2(byte - 127.0)
    codes = (blocks / scale).astype(np.float32).astype(dtype).astype(np.float64)
    return np.moveaxis((codes * scale).reshape(v.shape), -1, axis)


WIDE = False


def mx_kscale(k):
    if not WIDE:
        return np.ones(k)
    levels = np.array([10, -10, 5, -5, 0])
    if k % 512:
        return np.exp2(np.random.permutation(np.resize(levels, k // 32))).repeat(32)
    a = np.empty((k // 512, 16))
    for p in range(k // 512):
        a[p, :8] = np.random.permutation(np.resize(levels, 8))
        for g in range(8):
            far = levels[np.abs(levels - a[p, g]) >= 10]
            a[p, g + 8] = far[np.random.randint(len(far))]
    return np.exp2(a.ravel()).repeat(32)


def f64(x):
    return np.asarray(x).astype(np.float64)


def striped8(idx):
    return np.asarray(idx).reshape(8, -1, 16).transpose(0, 2, 1).reshape(128, -1).astype(np.uint16)


def unstriped8(offs):
    return offs.reshape(8, 16, -1).transpose(0, 2, 1).reshape(8, -1).astype(np.int64)


def pick8(x, idx, run):
    r = np.arange(len(x))
    return x[r[:, None], idx[r % (8 * run) // run]]


E2M1 = np.array([0.0, 0.5, 1.0, 1.5, 2.0, 3.0, 4.0, 6.0, -0.0, -0.5, -1.0, -1.5, -2.0, -3.0, -4.0, -6.0])


def pack_weight(w, fmt):
    k, n = w.shape
    w = f64(np.asarray(w, np.float32).astype(ml_dtypes.bfloat16)).reshape(k // 32, 32, n)
    amax = np.abs(w).max(1)
    if fmt == "e4m3":
        byte = np.frexp(amax)[1] - 1 + 127 - 7
    else:
        mant, ex = np.frexp(amax / 6.0)
        byte = np.where(mant > 0.5, ex, ex - 1) + 127
    byte = np.clip(np.where(amax > 0, byte, 1), 1, 254)
    scaled = (w * np.exp2(127.0 - byte)[:, None, :]).reshape(k, n).astype(np.float32)
    by_word = np.ascontiguousarray(scaled.reshape(k // 512, 128, 4, n).transpose(0, 1, 3, 2))
    if fmt == "e4m3":
        words = by_word.astype(ml_dtypes.float8_e4m3fn).view(np.uint8)
    else:
        c = by_word.astype(ml_dtypes.float4_e2m1fn).view(np.uint8) & 0xF
        words = (c[..., 0::2] | (c[..., 1::2] << 4)).reshape(k // 512, 128, 2 * n)
    return np.ascontiguousarray(words), np.ascontiguousarray(byte.astype(np.uint8).reshape(k // 512, 16, n))


def unpack_weight(words, scales, fmt):
    g, _, n = scales.shape
    words = np.ascontiguousarray(words).reshape(g, 128, n, -1)
    if fmt == "e4m3":
        vals = words.view(ml_dtypes.float8_e4m3fn).astype(np.float64)
    else:
        nib = np.empty((g, 128, n, 4), np.uint8)
        nib[..., 0::2] = words & 0xF
        nib[..., 1::2] = words >> 4
        vals = E2M1[nib]
    vals = vals * np.repeat(np.exp2(scales.astype(np.float64) - 127.0), 8, axis=1)[..., None]
    return vals.transpose(0, 1, 3, 2).reshape(g * 512, n)


def sigmoid(v):
    return 1.0 / (1.0 + np.exp(-v))


K, T, J, N, L = 512, 512, 512, 512, 512


def setup_inputs():
    n = np.random.standard_normal
    idx = np.stack([np.random.randint(0, T, J) for _ in range(8)])
    idx2 = np.stack([np.random.randint(0, T, J) for _ in range(8)])
    fk = mx_kscale(K)
    fl = mx_kscale(L)
    xtp = pack_weight(n((K, T)) / fk[:, None], "e4m3")
    wp = pack_weight(n((K, N)) * 1 / np.sqrt(K) * fk[:, None], "e2m1")
    wqp = pack_weight(n((L, N)) * 1 / np.sqrt(L) * fl[:, None], "e2m1")
    return {
        "xt_words": xtp[0],
        "xt_scales": xtp[1],
        "w_words": wp[0],
        "w_scales": wp[1],
        "qx": (n((L, J)) / fl[:, None]).astype(np.float32),
        "wq_words": wqp[0],
        "wq_scales": wqp[1],
        "offs": striped8(idx),
        "offs2": striped8(idx2),
    }


def reference(xt_words, xt_scales, w_words, w_scales, qx, wq_words, wq_scales, offs, offs2):
    idx = unstriped8(offs)
    idx2 = unstriped8(offs2)
    xtu = unpack_weight(xt_words, xt_scales, "e4m3")
    wu = unpack_weight(w_words, w_scales, "e2m1")
    wqu = unpack_weight(wq_words, wq_scales, "e2m1")
    z = wu.T @ xtu
    qxq = mxq(f64(qx), 0, "e4m3")
    g = wqu.T @ qxq
    y = pick8(z, idx2, 64) + sigmoid(g) * (pick8(z, idx, 64) - pick8(z, idx2, 64))
    return y

@@ -1,0 +1,152 @@
+from contextlib import ExitStack
+
+import concourse.mybir as mybir
+
+K, T, J, N, L = 512, 512, 512, 512, 512
+FLOPS = 2 * K * N * T + 2 * L * N * J
+
+F32 = mybir.dt.float32
+BF16 = mybir.dt.bfloat16
+I32 = mybir.dt.int32
+U32 = mybir.dt.uint32
+U16 = mybir.dt.uint16
+U8 = mybir.dt.uint8
+FP8X4 = mybir.dt.float8_e4m3fn_x4
+FP4X4 = mybir.dt.float4_e2m1fn_x4
+ACT = mybir.ActivationFunctionType
+ALU = mybir.AluOpType
+
+P = 128
+PACK = 4
+TILES = N // P
+HALF = J // 2
+RUN = 8
+
+
+def load_scale_rows(queue, plane, scales, quadrants):
+    for q in quadrants:
+        queue.dma_start(out=plane[32 * q : 32 * q + 4, :].bitcast(I32), in_=scales[0, 4 * q : 4 * q + 4, :].bitcast(I32))
+
+
+def tile_list_head_blend_two_lists_kernel(tc, xt_words, xt_scales, w_words, w_scales, qx, wq_words, wq_scales, offs, offs2, out):
+    nc = tc.nc
+    with ExitStack() as ctx:
+        keep = ctx.enter_context(tc.tile_pool(name="keep", bufs=1))
+        psum = ctx.enter_context(tc.psum_pool(name="psum", bufs=8))
+
+        list_a = keep.tile([P, J // 16], U16, name="list_a")
+        list_b = keep.tile([P, J // 16], U16, name="list_b")
+        w_plane = keep.tile([P, N], U8, name="w_plane", align_bytes=64)
+        x_plane = keep.tile([P, T], U8, name="x_plane", align_bytes=64)
+        wq_plane = keep.tile([P, N], U8, name="wq_plane", align_bytes=64)
+        w_raw = keep.tile([P, N], U16, name="w_raw", align_bytes=64)
+        wq_raw = keep.tile([P, N], U16, name="wq_raw", align_bytes=64)
+        x_codes = keep.tile([P, T], U32, name="x_codes", align_bytes=64)
+        q_raw = [keep.tile([P, PACK, HALF], F32, name=f"q_raw{h}", align_bytes=64) for h in range(2)]
+
+        load_scale_rows(nc.sync, w_plane, w_scales, range(4))
+        load_scale_rows(nc.sync, x_plane, xt_scales, (0,))
+        nc.sync.dma_start(out=w_raw[:].bitcast(I32), in_=w_words[0].bitcast(I32))
+        nc.sync.dma_start(out=x_codes[:].bitcast(I32), in_=xt_words[0].rearrange("p n t -> p (n t)").bitcast(I32))
+        q_rows = qx.rearrange("(p t) j -> p t j", t=PACK)
+        nc.sync.dma_start(out=q_raw[0][:], in_=q_rows[:, :, 0:HALF])
+        load_scale_rows(nc.sync, x_plane, xt_scales, (1, 2, 3))
+        load_scale_rows(nc.gpsimd, wq_plane, wq_scales, range(4))
+        nc.sync.dma_start(list_b[:], offs2)
+        nc.sync.dma_start(out=q_raw[1][:], in_=q_rows[:, :, HALF:J])
+        nc.sync.dma_start(list_a[:], offs)
+        nc.sync.dma_start(out=wq_raw[:].bitcast(I32), in_=wq_words[0].bitcast(I32))
+
+        def deal(raw, plane, name, rows_engine):
+            st = keep.tile([P, TILES, P], U8, name=f"{name}_scales", align_bytes=64)
+            for q in range(4):
+                rows = slice(32 * q, 32 * q + 4)
+                rows_engine.tensor_copy(out=st[rows, :, :].bitcast(I32).rearrange("p u (a r) -> p u a r", r=RUN // 4),
+                                      in_=plane[rows, :].bitcast(I32).rearrange("p (a u r) -> p u a r", u=TILES, r=RUN // 4))
+            wt = keep.tile([P, TILES, P], U16, name=f"{name}_words", align_bytes=64)
+            nc.vector.tensor_copy(out=wt[:].rearrange("p u (a r) -> p u a r", r=RUN),
+                                  in_=raw[:].rearrange("p (a u r) -> p u a r", u=TILES, r=RUN))
+            return [wt[:, u, :] for u in range(TILES)], [st[:, u, :] for u in range(TILES)]
+
+        w_cols, w_cols_scale = deal(w_raw, w_plane, "w", nc.vector)
+
+        z_acc = []
+        for u in range(TILES):
+            acc = psum.tile([P, T], F32, name="acc")
+            nc.tensor.matmul_mx(out=acc[:], lhsT=w_cols[u].bitcast(FP4X4), lhsT_scale=w_cols_scale[u],
+                                rhs=x_codes[:].bitcast(FP8X4), rhs_scale=x_plane[:], start=True, stop=True)
+            z_acc.append(acc)
+
+        q_codes = keep.tile([P, J], U32, name="q_codes", align_bytes=64)
+        q_plane = keep.tile([P, J], U8, name="q_plane", align_bytes=64)
+        grouped = [keep.tile([P, HALF, PACK], BF16, name=f"grouped{h}", align_bytes=64) for h in range(2)]
+
+        def cast(h):
+            nc.vector.tensor_copy(out=grouped[h][:].rearrange("p (c i) t -> p c t i", i=4),
+                                  in_=q_raw[h][:].rearrange("p t (c i) -> p c t i", i=4))
+
+        def quantise(h):
+            cols = slice(h * HALF, (h + 1) * HALF)
+            nc.vector.quantize_mx(out=q_codes[:, cols].bitcast(FP8X4), scales=q_plane[:, cols],
+                                  in_=grouped[h][:].rearrange("p c t -> p (c t)"))
+
+        cast(0)
+        wq_cols, wq_cols_scale = deal(wq_raw, wq_plane, "wq", nc.gpsimd)
+        quantise(0)
+        cast(1)
+
+        z = [keep.tile([P, T], F32, name=f"z{u}") for u in range(TILES)]
+        b = [keep.tile([P, J], F32, name=f"b{u}") for u in range(TILES)]
+        d = [keep.tile([P, J], F32, name=f"d{u}") for u in range(TILES)]
+        th = [keep.tile([P, J], F32, name=f"th{u}") for u in range(TILES)]
+        e = [keep.tile([P, J], F32, name=f"e{u}") for u in range(TILES)]
+        y = [keep.tile([P, J], F32, name=f"y{u}") for u in range(TILES)]
+        out_rows = out.rearrange("(a u r) j -> u a r j", u=TILES, r=RUN)
+
+        def fetch(u):
+            if u == 1:
+                nc.vector.tensor_copy(out=z[u][:], in_=z_acc[u][:])
+            else:
+                nc.scalar.activation(out=z[u][:], in_=z_acc[u][:], func=ACT.Copy)
+            for h in range(2):
+                cols = slice(h * HALF, (h + 1) * HALF)
+                ent = slice(h * HALF // 16, (h + 1) * HALF // 16)
+                nc.scalar.activation(out=b[u][:, cols], in_=z[u][:].indirect(list_b[:, ent]), func=ACT.Copy)
+
+        def diff(u, h):
+            cols = slice(h * HALF, (h + 1) * HALF)
+            ent = slice(h * HALF // 16, (h + 1) * HALF // 16)
+            nc.vector.tensor_tensor(d[u][:, cols], z[u][:].indirect(list_a[:, ent]), b[u][:, cols], ALU.subtract)
+
+        def gate(u):
+            acc = psum.tile([P, J], F32, name="acc")
+            nc.tensor.matmul_mx(out=acc[:], lhsT=wq_cols[u].bitcast(FP4X4), lhsT_scale=wq_cols_scale[u],
+                                rhs=q_codes[:].bitcast(FP8X4), rhs_scale=q_plane[:], start=True, stop=True)
+            nc.scalar.activation(out=th[u][:], in_=acc[:], func=ACT.Tanh, scale=0.5)
+
+        def weigh(u, cols):
+            nc.vector.scalar_tensor_tensor(out=e[u][:, cols], in0=th[u][:, cols], scalar=1.0, in1=d[u][:, cols], op0=ALU.add, op1=ALU.mult)
+
+        def blend(u, cols):
+            nc.vector.scalar_tensor_tensor(out=y[u][:, cols], in0=e[u][:, cols], scalar=0.5, in1=b[u][:, cols], op0=ALU.mult, op1=ALU.add)
+            nc.sync.dma_start(out=out_rows[u][:, :, cols], in_=y[u][:, cols])
+
+        whole = slice(0, J)
+        fetch(0)
+        diff(0, 0)
+        quantise(1)
+        diff(0, 1)
+        for u in range(1, TILES):
+            fetch(u)
+            gate(u - 1)
+            diff(u, 0)
+            weigh(u - 1, whole)
+            diff(u, 1)
+            blend(u - 1, whole)
+        last = TILES - 1
+        gate(last)
+        halves = [slice(0, HALF), slice(HALF, J)]
+        for cols in halves:
+            weigh(last, cols)
+        for cols in halves:
+            blend(last, cols)

@@ -32,54 +32,48 @@ def tile_list_head_blend_two_lists_kernel(tc, xt_words, xt_scales, w_words, w_sc
     nc = tc.nc
     with ExitStack() as ctx:
         keep = ctx.enter_context(tc.tile_pool(name="keep", bufs=1))
-        psum = ctx.enter_context(tc.psum_pool(name="psum", bufs=8))
+        psum = ctx.enter_context(tc.psum_pool(name="psum", bufs=1))
 
         list_a = keep.tile([P, J // 16], U16, name="list_a")
         list_b = keep.tile([P, J // 16], U16, name="list_b")
         w_plane = keep.tile([P, N], U8, name="w_plane", align_bytes=64)
         x_plane = keep.tile([P, T], U8, name="x_plane", align_bytes=64)
-        wq_plane = keep.tile([P, N], U8, name="wq_plane", align_bytes=64)
+        wq_plane = keep.tile([P, N], U8, name="wq_plane", tag="slot1", align_bytes=64)
         w_raw = keep.tile([P, N], U16, name="w_raw", align_bytes=64)
-        wq_raw = keep.tile([P, N], U16, name="wq_raw", align_bytes=64)
+        wq_raw = keep.tile([P, N], U16, name="wq_raw", tag="slot0", align_bytes=64)
         x_codes = keep.tile([P, T], U32, name="x_codes", align_bytes=64)
-        q_raw = [keep.tile([P, PACK, HALF], F32, name=f"q_raw{h}", align_bytes=64) for h in range(2)]
+        q_raw = [keep.tile([P, PACK, HALF], F32, name=f"q_raw{h}", tag=f"q_raw{h}", align_bytes=64) for h in range(2)]
 
+        nc.gpsimd.memset(wq_plane[:].bitcast(I32), 0)
+        q_rows = qx.rearrange("(p t) j -> p t j", t=PACK)
         load_scale_rows(nc.sync, w_plane, w_scales, range(4))
         load_scale_rows(nc.sync, x_plane, xt_scales, (0,))
         nc.sync.dma_start(out=w_raw[:].bitcast(I32), in_=w_words[0].bitcast(I32))
         nc.sync.dma_start(out=x_codes[:].bitcast(I32), in_=xt_words[0].rearrange("p n t -> p (n t)").bitcast(I32))
-        q_rows = qx.rearrange("(p t) j -> p t j", t=PACK)
         nc.sync.dma_start(out=q_raw[0][:], in_=q_rows[:, :, 0:HALF])
         load_scale_rows(nc.sync, x_plane, xt_scales, (1, 2, 3))
-        load_scale_rows(nc.gpsimd, wq_plane, wq_scales, range(4))
         nc.sync.dma_start(list_b[:], offs2)
         nc.sync.dma_start(out=q_raw[1][:], in_=q_rows[:, :, HALF:J])
-        nc.sync.dma_start(list_a[:], offs)
         nc.sync.dma_start(out=wq_raw[:].bitcast(I32), in_=wq_words[0].bitcast(I32))
+        nc.sync.dma_start(list_a[:], offs)
+        load_scale_rows(nc.sync, wq_plane, wq_scales, range(4))
 
-        def deal(raw, plane, name, rows_engine):
-            st = keep.tile([P, TILES, P], U8, name=f"{name}_scales", align_bytes=64)
-            for q in range(4):
-                rows = slice(32 * q, 32 * q + 4)
-                rows_engine.tensor_copy(out=st[rows, :, :].bitcast(I32).rearrange("p u (a r) -> p u a r", r=RUN // 4),
+        def deal(raw, plane, name, row_sets, words_tag, scales_tag):
+            st = keep.tile([P, TILES, P], U8, name=f"{name}_scales", tag=scales_tag, align_bytes=64)
+            for rows in row_sets:
+                nc.vector.tensor_copy(out=st[rows, :, :].bitcast(I32).rearrange("p u (a r) -> p u a r", r=RUN // 4),
                                       in_=plane[rows, :].bitcast(I32).rearrange("p (a u r) -> p u a r", u=TILES, r=RUN // 4))
-            wt = keep.tile([P, TILES, P], U16, name=f"{name}_words", align_bytes=64)
+            wt = keep.tile([P, TILES, P], U16, name=f"{name}_words", tag=words_tag, align_bytes=64)
             nc.vector.tensor_copy(out=wt[:].rearrange("p u (a r) -> p u a r", r=RUN),
                                   in_=raw[:].rearrange("p (a u r) -> p u a r", u=TILES, r=RUN))
             return [wt[:, u, :] for u in range(TILES)], [st[:, u, :] for u in range(TILES)]
 
-        w_cols, w_cols_scale = deal(w_raw, w_plane, "w", nc.vector)
+        w_cols, w_cols_scale = deal(w_raw, w_plane, "w", [slice(32 * q, 32 * q + 4) for q in range(4)], "w_words", "w_scales")
 
-        z_acc = []
-        for u in range(TILES):
-            acc = psum.tile([P, T], F32, name="acc")
-            nc.tensor.matmul_mx(out=acc[:], lhsT=w_cols[u].bitcast(FP4X4), lhsT_scale=w_cols_scale[u],
-                                rhs=x_codes[:].bitcast(FP8X4), rhs_scale=x_plane[:], start=True, stop=True)
-            z_acc.append(acc)
 
         q_codes = keep.tile([P, J], U32, name="q_codes", align_bytes=64)
         q_plane = keep.tile([P, J], U8, name="q_plane", align_bytes=64)
-        grouped = [keep.tile([P, HALF, PACK], BF16, name=f"grouped{h}", align_bytes=64) for h in range(2)]
+        grouped = [keep.tile([P, HALF, PACK], BF16, name=f"grouped{h}", tag=f"grouped{h}", align_bytes=64) for h in range(2)]
 
         def cast(h):
             nc.vector.tensor_copy(out=grouped[h][:].rearrange("p (c i) t -> p c t i", i=4),
@@ -91,62 +85,61 @@ def tile_list_head_blend_two_lists_kernel(tc, xt_words, xt_scales, w_words, w_sc
                                   in_=grouped[h][:].rearrange("p c t -> p (c t)"))
 
         cast(0)
-        wq_cols, wq_cols_scale = deal(wq_raw, wq_plane, "wq", nc.gpsimd)
         quantise(0)
         cast(1)
+        quantise(1)
+        wq_cols, wq_cols_scale = deal(wq_raw, wq_plane, "wq", [slice(0, P)], "q_raw1", "grouped1")
 
-        z = [keep.tile([P, T], F32, name=f"z{u}") for u in range(TILES)]
+        zy = [keep.tile([P, T + J], F32, name=f"zy{u}") for u in range(TILES)]
+        a = keep.tile([P, HALF], F32, name="a")
         b = [keep.tile([P, J], F32, name=f"b{u}") for u in range(TILES)]
-        d = [keep.tile([P, J], F32, name=f"d{u}") for u in range(TILES)]
+        d_first = keep.tile([P, J], F32, name="d_first", tag="slot0", align_bytes=64)
+        d_rest = keep.tile([P, TILES - 1, J], F32, name="d_rest", tag="slot1", align_bytes=64)
+        d = [d_first[:]] + [d_rest[:, u, :] for u in range(TILES - 1)]
         th = [keep.tile([P, J], F32, name=f"th{u}") for u in range(TILES)]
         e = [keep.tile([P, J], F32, name=f"e{u}") for u in range(TILES)]
-        y = [keep.tile([P, J], F32, name=f"y{u}") for u in range(TILES)]
         out_rows = out.rearrange("(a u r) j -> u a r j", u=TILES, r=RUN)
+        last = TILES - 1
 
         def fetch(u):
-            if u == 1:
-                nc.vector.tensor_copy(out=z[u][:], in_=z_acc[u][:])
-            else:
-                nc.scalar.activation(out=z[u][:], in_=z_acc[u][:], func=ACT.Copy)
-            for h in range(2):
-                cols = slice(h * HALF, (h + 1) * HALF)
-                ent = slice(h * HALF // 16, (h + 1) * HALF // 16)
-                nc.scalar.activation(out=b[u][:, cols], in_=z[u][:].indirect(list_b[:, ent]), func=ACT.Copy)
+            acc = psum.tile([P, T], F32, name="z_acc", tag="bank_g0" if u == last else f"bank_z{u}")
+            nc.tensor.matmul_mx(out=acc[:], lhsT=w_cols[u].bitcast(FP4X4), lhsT_scale=w_cols_scale[u],
+                                rhs=x_codes[:].bitcast(FP8X4), rhs_scale=x_plane[:], start=True, stop=True)
+            nc.scalar.activation(out=zy[u][:, 0:T], in_=acc[:], func=ACT.Copy)
+            nc.scalar.activation(out=b[u][:], in_=zy[u][:].indirect(list_b[:]), func=ACT.Copy)
 
-        def diff(u, h):
-            cols = slice(h * HALF, (h + 1) * HALF)
-            ent = slice(h * HALF // 16, (h + 1) * HALF // 16)
-            nc.vector.tensor_tensor(d[u][:, cols], z[u][:].indirect(list_a[:, ent]), b[u][:, cols], ALU.subtract)
+        def diff(u):
+            if u == last:
+                nc.vector.tensor_tensor(d[u][:, 0:HALF], zy[u][:].indirect(list_a[:, 0 : HALF // 16]), b[u][:, 0:HALF], ALU.subtract)
+                nc.scalar.activation(out=a[:], in_=zy[u][:].indirect(list_a[:, HALF // 16 : J // 16]), func=ACT.Copy)
+                nc.vector.tensor_tensor(d[u][:, HALF:J], a[:], b[u][:, HALF:J], ALU.subtract)
+            else:
+                nc.vector.tensor_tensor(d[u], zy[u][:].indirect(list_a[:]), b[u][:], ALU.subtract)
 
         def gate(u):
-            acc = psum.tile([P, J], F32, name="acc")
+            acc = psum.tile([P, J], F32, name="g_acc", tag=f"bank_g{u}")
             nc.tensor.matmul_mx(out=acc[:], lhsT=wq_cols[u].bitcast(FP4X4), lhsT_scale=wq_cols_scale[u],
                                 rhs=q_codes[:].bitcast(FP8X4), rhs_scale=q_plane[:], start=True, stop=True)
             nc.scalar.activation(out=th[u][:], in_=acc[:], func=ACT.Tanh, scale=0.5)
 
-        def weigh(u, cols):
-            nc.vector.scalar_tensor_tensor(out=e[u][:, cols], in0=th[u][:, cols], scalar=1.0, in1=d[u][:, cols], op0=ALU.add, op1=ALU.mult)
+        def weigh(u, lo, hi):
+            nc.vector.scalar_tensor_tensor(out=e[u][:, lo:hi], in0=th[u][:, lo:hi], scalar=1.0, in1=d[u][:, lo:hi], op0=ALU.add, op1=ALU.mult)
 
-        def blend(u, cols):
-            nc.vector.scalar_tensor_tensor(out=y[u][:, cols], in0=e[u][:, cols], scalar=0.5, in1=b[u][:, cols], op0=ALU.mult, op1=ALU.add)
-            nc.sync.dma_start(out=out_rows[u][:, :, cols], in_=y[u][:, cols])
+        def blend(u, lo, hi):
+            y = zy[u][:, T + lo : T + hi]
+            nc.vector.scalar_tensor_tensor(out=y, in0=e[u][:, lo:hi], scalar=0.5, in1=b[u][:, lo:hi], op0=ALU.mult, op1=ALU.add)
+            nc.sync.dma_start(out=out_rows[u][:, :, lo:hi], in_=y)
 
-        whole = slice(0, J)
         fetch(0)
-        diff(0, 0)
-        quantise(1)
-        diff(0, 1)
+        diff(0)
         for u in range(1, TILES):
             fetch(u)
             gate(u - 1)
-            diff(u, 0)
-            weigh(u - 1, whole)
-            diff(u, 1)
-            blend(u - 1, whole)
-        last = TILES - 1
+            weigh(u - 1, 0, J)
+            diff(u)
+            blend(u - 1, 0, J)
         gate(last)
-        halves = [slice(0, HALF), slice(HALF, J)]
-        for cols in halves:
-            weigh(last, cols)
-        for cols in halves:
-            blend(last, cols)
+        for lo in (0, HALF):
+            weigh(last, lo, lo + HALF)
+        for lo in (0, HALF):
+            blend(last, lo, lo + HALF)

@@ -55,8 +55,8 @@ def tile_list_head_blend_two_lists_kernel(tc, xt_words, xt_scales, w_words, w_sc
         nc.sync.dma_start(list_b[:], offs2)
         nc.sync.dma_start(out=q_raw[1][:], in_=q_rows[:, :, HALF:J])
         nc.sync.dma_start(out=wq_raw[:].bitcast(I32), in_=wq_words[0].bitcast(I32))
-        nc.sync.dma_start(list_a[:], offs)
         load_scale_rows(nc.sync, wq_plane, wq_scales, range(4))
+        nc.sync.dma_start(list_a[:], offs)
 
         def deal(raw, plane, name, row_sets, words_tag, scales_tag):
             st = keep.tile([P, TILES, P], U8, name=f"{name}_scales", tag=scales_tag, align_bytes=64)
@@ -91,28 +91,34 @@ def tile_list_head_blend_two_lists_kernel(tc, xt_words, xt_scales, w_words, w_sc
         wq_cols, wq_cols_scale = deal(wq_raw, wq_plane, "wq", [slice(0, P)], "q_raw1", "grouped1")
 
         zy = [keep.tile([P, T + J], F32, name=f"zy{u}") for u in range(TILES)]
-        a = keep.tile([P, HALF], F32, name="a")
+        a = keep.tile([P, J], F32, name="a")
         b = [keep.tile([P, J], F32, name=f"b{u}") for u in range(TILES)]
-        d_first = keep.tile([P, J], F32, name="d_first", tag="slot0", align_bytes=64)
-        d_rest = keep.tile([P, TILES - 1, J], F32, name="d_rest", tag="slot1", align_bytes=64)
-        d = [d_first[:]] + [d_rest[:, u, :] for u in range(TILES - 1)]
+        d_all = keep.tile([P, TILES, J], F32, name="d_all", tag="slot1", align_bytes=64)
+        d = [d_all[:, u, :] for u in range(TILES)]
         th = [keep.tile([P, J], F32, name=f"th{u}") for u in range(TILES)]
         e = [keep.tile([P, J], F32, name=f"e{u}") for u in range(TILES)]
         out_rows = out.rearrange("(a u r) j -> u a r j", u=TILES, r=RUN)
         last = TILES - 1
 
-        def fetch(u):
-            acc = psum.tile([P, T], F32, name="z_acc", tag="bank_g0" if u == last else f"bank_z{u}")
+        def features(u, lo, hi, bank):
+            acc = psum.tile([P, hi - lo], F32, name="z_acc", tag=bank)
             nc.tensor.matmul_mx(out=acc[:], lhsT=w_cols[u].bitcast(FP4X4), lhsT_scale=w_cols_scale[u],
-                                rhs=x_codes[:].bitcast(FP8X4), rhs_scale=x_plane[:], start=True, stop=True)
-            nc.scalar.activation(out=zy[u][:, 0:T], in_=acc[:], func=ACT.Copy)
+                                rhs=x_codes[:, lo:hi].bitcast(FP8X4), rhs_scale=x_plane[:, lo:hi], start=True, stop=True)
+            return acc
+
+        def fetch(u):
+            if u == 0:
+                nc.scalar.activation(out=zy[u][:, 0:HALF], in_=features(u, 0, HALF, "bank_z0a")[:], func=ACT.Copy)
+                nc.scalar.activation(out=zy[u][:, HALF:T], in_=features(u, HALF, T, "bank_z0b")[:], func=ACT.Copy)
+            else:
+                bank = "bank_z1" if u == 1 else f"bank_g{u - 2}"
+                nc.scalar.activation(out=zy[u][:, 0:T], in_=features(u, 0, T, bank)[:], func=ACT.Copy)
             nc.scalar.activation(out=b[u][:], in_=zy[u][:].indirect(list_b[:]), func=ACT.Copy)
 
         def diff(u):
             if u == last:
-                nc.vector.tensor_tensor(d[u][:, 0:HALF], zy[u][:].indirect(list_a[:, 0 : HALF // 16]), b[u][:, 0:HALF], ALU.subtract)
-                nc.scalar.activation(out=a[:], in_=zy[u][:].indirect(list_a[:, HALF // 16 : J // 16]), func=ACT.Copy)
-                nc.vector.tensor_tensor(d[u][:, HALF:J], a[:], b[u][:, HALF:J], ALU.subtract)
+                nc.scalar.activation(out=a[:], in_=zy[u][:].indirect(list_a[:]), func=ACT.Copy)
+                nc.vector.tensor_tensor(d[u], a[:], b[u][:], ALU.subtract)
             else:
                 nc.vector.tensor_tensor(d[u], zy[u][:].indirect(list_a[:]), b[u][:], ALU.subtract)
 
@@ -120,7 +126,8 @@ def tile_list_head_blend_two_lists_kernel(tc, xt_words, xt_scales, w_words, w_sc
             acc = psum.tile([P, J], F32, name="g_acc", tag=f"bank_g{u}")
             nc.tensor.matmul_mx(out=acc[:], lhsT=wq_cols[u].bitcast(FP4X4), lhsT_scale=wq_cols_scale[u],
                                 rhs=q_codes[:].bitcast(FP8X4), rhs_scale=q_plane[:], start=True, stop=True)
-            nc.scalar.activation(out=th[u][:], in_=acc[:], func=ACT.Tanh, scale=0.5)
+            for lo, hi in ((0, HALF), (HALF, J)) if u == last else ((0, J),):
+                nc.scalar.activation(out=th[u][:, lo:hi], in_=acc[:, lo:hi], func=ACT.Tanh, scale=0.5)
 
         def weigh(u, lo, hi):
             nc.vector.scalar_tensor_tensor(out=e[u][:, lo:hi], in0=th[u][:, lo:hi], scalar=1.0, in1=d[u][:, lo:hi], op0=ALU.add, op1=ALU.mult)
@@ -131,12 +138,14 @@ def tile_list_head_blend_two_lists_kernel(tc, xt_words, xt_scales, w_words, w_sc
             nc.sync.dma_start(out=out_rows[u][:, :, lo:hi], in_=y)
 
         fetch(0)
+        fetch(1)
         diff(0)
         for u in range(1, TILES):
-            fetch(u)
             gate(u - 1)
-            weigh(u - 1, 0, J)
             diff(u)
+            if u < last:
+                fetch(u + 1)
+            weigh(u - 1, 0, J)
             blend(u - 1, 0, J)
         gate(last)
         for lo in (0, HALF):

@@ -91,7 +91,7 @@ def tile_list_head_blend_two_lists_kernel(tc, xt_words, xt_scales, w_words, w_sc
         wq_cols, wq_cols_scale = deal(wq_raw, wq_plane, "wq", [slice(0, P)], "q_raw1", "grouped1")
 
         zy = [keep.tile([P, T + J], F32, name=f"zy{u}") for u in range(TILES)]
-        a = keep.tile([P, J], F32, name="a")
+        a = keep.tile([P, HALF], F32, name="a")
         b = [keep.tile([P, J], F32, name=f"b{u}") for u in range(TILES)]
         d_all = keep.tile([P, TILES, J], F32, name="d_all", tag="slot1", align_bytes=64)
         d = [d_all[:, u, :] for u in range(TILES)]
@@ -115,15 +115,16 @@ def tile_list_head_blend_two_lists_kernel(tc, xt_words, xt_scales, w_words, w_sc
                 nc.scalar.activation(out=zy[u][:, 0:T], in_=features(u, 0, T, bank)[:], func=ACT.Copy)
             nc.scalar.activation(out=b[u][:], in_=zy[u][:].indirect(list_b[:]), func=ACT.Copy)
 
-        def diff(u):
-            if u == last:
-                nc.scalar.activation(out=a[:], in_=zy[u][:].indirect(list_a[:]), func=ACT.Copy)
-                nc.vector.tensor_tensor(d[u], a[:], b[u][:], ALU.subtract)
-            else:
-                nc.vector.tensor_tensor(d[u], zy[u][:].indirect(list_a[:]), b[u][:], ALU.subtract)
+        def diff(u, lo, hi):
+            entries = list_a[:, lo // 16 : hi // 16]
+            nc.vector.tensor_tensor(d[u][:, lo:hi], zy[u][:].indirect(entries), b[u][:, lo:hi], ALU.subtract)
+
+        def diff_split(u, lo, hi):
+            nc.scalar.activation(out=a[:], in_=zy[u][:].indirect(list_a[:, lo // 16 : hi // 16]), func=ACT.Copy)
+            nc.vector.tensor_tensor(d[u][:, lo:hi], a[:], b[u][:, lo:hi], ALU.subtract)
 
         def gate(u):
-            acc = psum.tile([P, J], F32, name="g_acc", tag=f"bank_g{u}")
+            acc = psum.tile([P, J], F32, name="g_acc", tag="bank_g1" if u == last else f"bank_g{u}")
             nc.tensor.matmul_mx(out=acc[:], lhsT=wq_cols[u].bitcast(FP4X4), lhsT_scale=wq_cols_scale[u],
                                 rhs=q_codes[:].bitcast(FP8X4), rhs_scale=q_plane[:], start=True, stop=True)
             for lo, hi in ((0, HALF), (HALF, J)) if u == last else ((0, J),):
@@ -139,15 +140,23 @@ def tile_list_head_blend_two_lists_kernel(tc, xt_words, xt_scales, w_words, w_sc
 
         fetch(0)
         fetch(1)
-        diff(0)
-        for u in range(1, TILES):
-            gate(u - 1)
-            diff(u)
-            if u < last:
-                fetch(u + 1)
-            weigh(u - 1, 0, J)
-            blend(u - 1, 0, J)
-        gate(last)
+        diff(0, 0, J)
+        gate(0)
+        diff(1, 0, J)
+        gate(1)
+        fetch(2)
+        gate(2)
+        fetch(3)
+        weigh(0, 0, J)
+        weigh(1, 0, J)
+        blend(0, 0, J)
+        diff(2, 0, J)
+        blend(1, 0, J)
+        weigh(2, 0, J)
+        diff(3, 0, HALF)
+        blend(2, 0, J)
+        diff_split(3, HALF, J)
+        gate(3)
         for lo in (0, HALF):
             weigh(last, lo, lo + HALF)
         for lo in (0, HALF):

from contextlib import ExitStack

import concourse.mybir as mybir

K, T, J, N, L = 512, 512, 512, 512, 512
FLOPS = 2 * K * N * T + 2 * L * N * J

F32 = mybir.dt.float32
BF16 = mybir.dt.bfloat16
I32 = mybir.dt.int32
U32 = mybir.dt.uint32
U16 = mybir.dt.uint16
U8 = mybir.dt.uint8
FP8X4 = mybir.dt.float8_e4m3fn_x4
FP4X4 = mybir.dt.float4_e2m1fn_x4
ACT = mybir.ActivationFunctionType
ALU = mybir.AluOpType

P = 128
PACK = 4
TILES = N // P
HALF = J // 2
RUN = 8


def load_scale_rows(queue, plane, scales, quadrants):
    for q in quadrants:
        queue.dma_start(out=plane[32 * q : 32 * q + 4, :].bitcast(I32), in_=scales[0, 4 * q : 4 * q + 4, :].bitcast(I32))


def tile_list_head_blend_two_lists_kernel(tc, xt_words, xt_scales, w_words, w_scales, qx, wq_words, wq_scales, offs, offs2, out):
    nc = tc.nc
    with ExitStack() as ctx:
        keep = ctx.enter_context(tc.tile_pool(name="keep", bufs=1))
        psum = ctx.enter_context(tc.psum_pool(name="psum", bufs=1))

        list_a = keep.tile([P, J // 16], U16, name="list_a")
        list_b = keep.tile([P, J // 16], U16, name="list_b")
        w_plane = keep.tile([P, N], U8, name="w_plane", align_bytes=64)
        x_plane = keep.tile([P, T], U8, name="x_plane", align_bytes=64)
        wq_plane = keep.tile([P, N], U8, name="wq_plane", tag="slot1", align_bytes=64)
        w_raw = keep.tile([P, N], U16, name="w_raw", align_bytes=64)
        wq_raw = keep.tile([P, N], U16, name="wq_raw", tag="slot0", align_bytes=64)
        x_codes = keep.tile([P, T], U32, name="x_codes", align_bytes=64)
        q_raw = [keep.tile([P, PACK, HALF], F32, name=f"q_raw{h}", tag=f"q_raw{h}", align_bytes=64) for h in range(2)]

        nc.gpsimd.memset(wq_plane[:].bitcast(I32), 0)
        q_rows = qx.rearrange("(p t) j -> p t j", t=PACK)
        load_scale_rows(nc.sync, w_plane, w_scales, range(4))
        load_scale_rows(nc.sync, x_plane, xt_scales, (0,))
        nc.sync.dma_start(out=w_raw[:].bitcast(I32), in_=w_words[0].bitcast(I32))
        nc.sync.dma_start(out=x_codes[:].bitcast(I32), in_=xt_words[0].rearrange("p n t -> p (n t)").bitcast(I32))
        nc.sync.dma_start(out=q_raw[0][:], in_=q_rows[:, :, 0:HALF])
        load_scale_rows(nc.sync, x_plane, xt_scales, (1, 2, 3))
        nc.sync.dma_start(list_b[:], offs2)
        nc.sync.dma_start(out=q_raw[1][:], in_=q_rows[:, :, HALF:J])
        nc.sync.dma_start(out=wq_raw[:].bitcast(I32), in_=wq_words[0].bitcast(I32))
        load_scale_rows(nc.sync, wq_plane, wq_scales, range(4))
        nc.sync.dma_start(list_a[:], offs)

        def deal(raw, plane, name, row_sets, words_tag, scales_tag):
            st = keep.tile([P, TILES, P], U8, name=f"{name}_scales", tag=scales_tag, align_bytes=64)
            for rows in row_sets:
                nc.vector.tensor_copy(out=st[rows, :, :].bitcast(I32).rearrange("p u (a r) -> p u a r", r=RUN // 4),
                                      in_=plane[rows, :].bitcast(I32).rearrange("p (a u r) -> p u a r", u=TILES, r=RUN // 4))
            wt = keep.tile([P, TILES, P], U16, name=f"{name}_words", tag=words_tag, align_bytes=64)
            nc.vector.tensor_copy(out=wt[:].rearrange("p u (a r) -> p u a r", r=RUN),
                                  in_=raw[:].rearrange("p (a u r) -> p u a r", u=TILES, r=RUN))
            return [wt[:, u, :] for u in range(TILES)], [st[:, u, :] for u in range(TILES)]

        w_cols, w_cols_scale = deal(w_raw, w_plane, "w", [slice(32 * q, 32 * q + 4) for q in range(4)], "w_words", "w_scales")


        q_codes = keep.tile([P, J], U32, name="q_codes", align_bytes=64)
        q_plane = keep.tile([P, J], U8, name="q_plane", align_bytes=64)
        grouped = [keep.tile([P, HALF, PACK], BF16, name=f"grouped{h}", tag=f"grouped{h}", align_bytes=64) for h in range(2)]

        def cast(h):
            nc.vector.tensor_copy(out=grouped[h][:].rearrange("p (c i) t -> p c t i", i=4),
                                  in_=q_raw[h][:].rearrange("p t (c i) -> p c t i", i=4))

        def quantise(h):
            cols = slice(h * HALF, (h + 1) * HALF)
            nc.vector.quantize_mx(out=q_codes[:, cols].bitcast(FP8X4), scales=q_plane[:, cols],
                                  in_=grouped[h][:].rearrange("p c t -> p (c t)"))

        cast(0)
        quantise(0)
        cast(1)
        quantise(1)
        wq_cols, wq_cols_scale = deal(wq_raw, wq_plane, "wq", [slice(0, P)], "q_raw1", "grouped1")

        zy = [keep.tile([P, T + J], F32, name=f"zy{u}") for u in range(TILES)]
        a = keep.tile([P, HALF], F32, name="a")
        b = [keep.tile([P, J], F32, name=f"b{u}") for u in range(TILES)]
        d_all = keep.tile([P, TILES, J], F32, name="d_all", tag="slot1", align_bytes=64)
        d = [d_all[:, u, :] for u in range(TILES)]
        th = [keep.tile([P, J], F32, name=f"th{u}") for u in range(TILES)]
        e = [keep.tile([P, J], F32, name=f"e{u}") for u in range(TILES)]
        out_rows = out.rearrange("(a u r) j -> u a r j", u=TILES, r=RUN)
        last = TILES - 1

        def features(u, lo, hi, bank):
            acc = psum.tile([P, hi - lo], F32, name="z_acc", tag=bank)
            nc.tensor.matmul_mx(out=acc[:], lhsT=w_cols[u].bitcast(FP4X4), lhsT_scale=w_cols_scale[u],
                                rhs=x_codes[:, lo:hi].bitcast(FP8X4), rhs_scale=x_plane[:, lo:hi], start=True, stop=True)
            return acc

        def fetch(u):
            if u == 0:
                nc.scalar.activation(out=zy[u][:, 0:HALF], in_=features(u, 0, HALF, "bank_z0a")[:], func=ACT.Copy)
                nc.scalar.activation(out=zy[u][:, HALF:T], in_=features(u, HALF, T, "bank_z0b")[:], func=ACT.Copy)
            else:
                bank = "bank_z1" if u == 1 else f"bank_g{u - 2}"
                nc.scalar.activation(out=zy[u][:, 0:T], in_=features(u, 0, T, bank)[:], func=ACT.Copy)
            nc.scalar.activation(out=b[u][:], in_=zy[u][:].indirect(list_b[:]), func=ACT.Copy)

        def diff(u, lo, hi):
            entries = list_a[:, lo // 16 : hi // 16]
            nc.vector.tensor_tensor(d[u][:, lo:hi], zy[u][:].indirect(entries), b[u][:, lo:hi], ALU.subtract)

        def diff_split(u, lo, hi):
            nc.scalar.activation(out=a[:], in_=zy[u][:].indirect(list_a[:, lo // 16 : hi // 16]), func=ACT.Copy)
            nc.vector.tensor_tensor(d[u][:, lo:hi], a[:], b[u][:, lo:hi], ALU.subtract)

        def gate(u):
            acc = psum.tile([P, J], F32, name="g_acc", tag="bank_g1" if u == last else f"bank_g{u}")
            nc.tensor.matmul_mx(out=acc[:], lhsT=wq_cols[u].bitcast(FP4X4), lhsT_scale=wq_cols_scale[u],
                                rhs=q_codes[:].bitcast(FP8X4), rhs_scale=q_plane[:], start=True, stop=True)
            for lo, hi in ((0, HALF), (HALF, J)) if u == last else ((0, J),):
                nc.scalar.activation(out=th[u][:, lo:hi], in_=acc[:, lo:hi], func=ACT.Tanh, scale=0.5)

        def weigh(u, lo, hi):
            nc.vector.scalar_tensor_tensor(out=e[u][:, lo:hi], in0=th[u][:, lo:hi], scalar=1.0, in1=d[u][:, lo:hi], op0=ALU.add, op1=ALU.mult)

        def blend(u, lo, hi):
            y = zy[u][:, T + lo : T + hi]
            nc.vector.scalar_tensor_tensor(out=y, in0=e[u][:, lo:hi], scalar=0.5, in1=b[u][:, lo:hi], op0=ALU.mult, op1=ALU.add)
            nc.sync.dma_start(out=out_rows[u][:, :, lo:hi], in_=y)

        fetch(0)
        fetch(1)
        diff(0, 0, J)
        gate(0)
        diff(1, 0, J)
        gate(1)
        fetch(2)
        gate(2)
        fetch(3)
        weigh(0, 0, J)
        weigh(1, 0, J)
        blend(0, 0, J)
        diff(2, 0, J)
        blend(1, 0, J)
        weigh(2, 0, J)
        diff(3, 0, HALF)
        blend(2, 0, J)
        diff_split(3, HALF, J)
        gate(3)
        for lo in (0, HALF):
            weigh(last, lo, lo + HALF)
        for lo in (0, HALF):
            blend(last, lo, lo + HALF)
